import numpy as np, ml_dtypes
CORES = [24,25,26,27,48,49,50,51,72,73,74,75,96,97,98,99]
N = 16
import mx_ref
NC, G, KO, SH = 128, 4, 2, 1
C = np.float32(0.019)
BF = ml_dtypes.bfloat16
def cut(t, i, w=512):
    return t[:, w * i:w * i + w]
def tile(rs):
    return np.stack(rs, axis=2).reshape(128, -1).astype(BF)
def layer(w, X):
    out = []
    for i in range(G):
        for t in range(len(X)):
            p = mx_ref.matmul(mx_ref.quantize(cut(w, len(X) * i + t)), X[t])
            z = p if t == 0 else z + p
        out.append(z)
    return out
def act(Z):
    return [np.maximum(z, 0) * C for z in Z]
def inputs(rng, e, E):
    def f(*shape):
        v = (rng.standard_normal(shape, dtype=np.float32) * np.exp2(rng.integers(-2, 3, shape[:-1] + (1,)))).astype(BF)
        return mx_ref.spread((v.astype(np.float32) * np.exp2(rng.integers(-E, E + 1, shape[:-2] + (1, 1))).astype(np.float32)).astype(BF), rng, e)
    def packed(k):
        c = np.zeros((N, 128, k * 512), np.uint8); s = np.zeros((N, 128, k * 128), np.uint8)
        for r in range(N):
            for i in range(k):
                a, b = mx_ref.quantize(f(128, 512)); c[r][:, 512 * i:512 * i + 512] = a; s[r][:, 128 * i:128 * i + 128] = mx_ref.plane(b, rng)
        return c, s
    d = {}
    d["kc"], d["ks"] = packed(KO)
    d["x"] = f(N, 128, 4 * NC)
    d["wk"] = f(N, 128, G * 512)
    d["q"] = f(N, 128, 512)
    return d
def setup_inputs(rng):
    return inputs(rng, 0, 0)
def setup_inputs_blocks(rng):
    return inputs(rng, 4, 0)
def setup_inputs_wide(rng):
    return inputs(rng, 0, 8)
def reference(kc, ks, x, wk, q):
    new = [mx_ref.quantize(tile(act(layer(wk[r], [mx_ref.quantize(x[r])])))) for r in range(N)]
    y = np.zeros((N, 128, 128 * KO + NC), np.float32)
    for o in range(N):
        old = (np.ascontiguousarray(kc[o]), mx_ref.live(ks[o]))
        qq = mx_ref.quantize(q[o])
        y[o] = np.concatenate([mx_ref.matmul(qq, old), mx_ref.matmul(qq, new[(o - SH) % N])], axis=1)
    return {"y": y}

from concourse.mybir import dt, AluOpType, ActivationFunctionType

NC = 128
KEYS = 256
W = 512
G = 4
SCALE = 0.019
ENGINES = 8

SCRATCH = {
    "xt": ("sbuf", [128, W], "bfloat16"),
    "wt": ("sbuf", [128, G * W], "bfloat16"),
    "qt": ("sbuf", [128, W], "bfloat16"),
    "kt": ("sbuf", [128, W], "bfloat16"),
    "xc": ("sbuf", [128, NC], "float8_e4m3fn_x4"),
    "xs": ("sbuf", [128, NC], "uint8"),
    "wc": ("sbuf", [128, G * 128], "float8_e4m3fn_x4"),
    "ws": ("sbuf", [128, G * 128], "uint8"),
    "qc": ("sbuf", [128, 128], "float8_e4m3fn_x4"),
    "qs": ("sbuf", [128, 128], "uint8"),
    "old_c": ("sbuf", [128, KEYS], "float8_e4m3fn_x4"),
    "old_s": ("sbuf", [128, KEYS], "uint8"),
    "new_c": ("sbuf", [128, NC], "float8_e4m3fn_x4"),
    "new_s": ("sbuf", [128, NC], "uint8"),
    "land_c": ("sbuf", [128, NC], "float8_e4m3fn_x4"),
    "land_s": ("sbuf", [128, NC], "uint8"),
    "yo": ("sbuf", [128, KEYS], "float32"),
    "yn": ("sbuf", [128, NC], "float32"),
    "pz": ("psum", [128, 512 * G], "float32"),
    "po": ("psum", [128, 512], "float32"),
    "pn": ("psum", [128, 512], "float32"),
}
SEMAPHORES = (["ldx", "ldq", "ldk", "qx", "qk", "qq", "rel", "last", "mo", "mn", "co", "cn", "sto", "stn", "sent", "arrived"]
              + ["ldw%d" % i for i in range(G)] + ["qw%d" % i for i in range(G)] + ["mz%d" % i for i in range(G)])


def lowest(mask, n):
    out = 0
    for b in range(mask.bit_length()):
        if mask >> b & 1 and n > 0:
            out |= 1 << b
            n -= 1
    return out


def rank_program(g, core, T, topo):
    rank = T.rank_of(core)
    if rank is None:
        return
    S = T.sem
    dst = T.cores[(rank + 1) % len(T.cores)]
    rid, pid, _ = topo.addr(dst)
    eng = lowest(topo.mask(core, dst), ENGINES)
    relu = ActivationFunctionType.Relu

    def wcols(i):
        return slice(W * i, W * (i + 1))

    def tcols(i):
        return slice(128 * i, 128 * (i + 1))

    g.sync.dma_start(T.xt[:, :], T.x[:, :]).then_inc(S.ldx, 16)
    for i in (1, 3):
        g.sync.dma_start(T.wt[:, wcols(i)], T.wk[:, wcols(i)]).then_inc(S["ldw%d" % i], 16)
    for i in (0, 2):
        g.scalar.dma_start(T.wt[:, wcols(i)], T.wk[:, wcols(i)]).then_inc(S["ldw%d" % i], 16)
    g.sync.wait_ge(S.ldx, 16)
    g.sync.dma_start(T.qt[:, :], T.q[:, :]).then_inc(S.ldq, 16)
    g.sync.dma_start(T.old_c[:, :].bitcast(dt.uint8), T.kc[:, :]).then_inc(S.ldk, 16)
    g.sync.dma_start(T.old_s[:, :], T.ks[:, :]).then_inc(S.ldk, 16)

    v = g.vector
    v.wait_ge(S.ldx, 16)
    v.quantize_mx(T.xc[:, :], T.xs[:, :], T.xt[:, :]).then_inc(S.qx, 1)
    for i in range(G):
        v.wait_ge(S["ldw%d" % i], 16)
        v.quantize_mx(T.wc[:, tcols(i)], T.ws[:, tcols(i)], T.wt[:, wcols(i)]).then_inc(S["qw%d" % i], 1)
    b = G - 1
    v.wait_ge(S["mz%d" % b], 1)
    v.tensor_scalar(T.kt[:, b:W:4], T.pz[:, 512 * b:512 * b + NC], 0.0, SCALE, AluOpType.max, AluOpType.mult).then_inc(S.last, 1)
    v.wait_ge(S.rel, G - 1)
    v.wait_ge(S.last, 1)
    v.quantize_mx(T.new_c[:, :], T.new_s[:, :], T.kt[:, :]).then_inc(S.qk, 1)
    v.wait_ge(S.ldq, 16)
    v.quantize_mx(T.qc[:, :], T.qs[:, :], T.qt[:, :]).then_inc(S.qq, 1)
    v.wait_ge(S.mn, 1)
    v.tensor_copy(T.yn[:, :], T.pn[:, 0:NC]).then_inc(S.cn, 1)

    t = g.tensor
    t.wait_ge(S.qx, 1)
    for i in range(G):
        t.wait_ge(S["qw%d" % i], 1)
        t.matmul_mx(T.pz[:, 512 * i:512 * i + NC], T.wc[:, tcols(i)], T.ws[:, tcols(i)], T.xc[:, :], T.xs[:, :], True, True).then_inc(S["mz%d" % i], 1)
    t.wait_ge(S.qq, 1)
    t.wait_ge(S.ldk, 32)
    t.matmul_mx(T.po[:, 0:KEYS], T.qc[:, :], T.qs[:, :], T.old_c[:, :], T.old_s[:, :], True, True).then_inc(S.mo, 1)
    t.wait_ge(S.arrived, 2 * ENGINES)
    t.matmul_mx(T.pn[:, 0:NC], T.qc[:, :], T.qs[:, :], T.land_c[:, :], T.land_s[:, :], True, True).then_inc(S.mn, 1)

    for i in range(G - 1):
        g.scalar.wait_ge(S["mz%d" % i], 1)
        g.scalar.activation(T.kt[:, i:W:4], T.pz[:, 512 * i:512 * i + NC], relu, scale=SCALE).then_inc(S.rel, 1)
    g.scalar.wait_ge(S.mo, 1)
    g.scalar.activation(T.yo[:, :], T.po[:, 0:KEYS], ActivationFunctionType.Copy).then_inc(S.co, 1)
    g.scalar.wait_ge(S.co, 1)
    g.scalar.dma_start(T.y[:, 0:KEYS], T.yo[:, :]).then_inc(S.sto, 16)

    g.wait_ge(S.qk, 1)
    g.remote_dma(T.land_c[:, :].bitcast(dt.uint8), T.new_c[:, :].bitcast(dt.uint8), S.arrived, S.sent, pid, rid, eng)
    g.remote_dma(T.land_s[:, :], T.new_s[:, :], S.arrived, S.sent, pid, rid, eng)
    g.wait_ge(S.sent, 2 * ENGINES)

    g.sync.wait_ge(S.cn, 1)
    g.sync.dma_start(T.y[:, KEYS:KEYS + NC], T.yn[:, :]).then_inc(S.stn, 16)
    g.scalar.wait_ge(S.sto, 16)
    g.sync.wait_ge(S.stn, 16)
